import numpy as np
import ml_dtypes


def mxq(x, axis, fmt="e4m3"):
    dtype, down = {"e4m3": (ml_dtypes.float8_e4m3fn, 7), "e5m2": (ml_dtypes.float8_e5m2, 14)}[fmt]
    v = np.moveaxis(np.asarray(x, np.float32).astype(ml_dtypes.bfloat16).astype(np.float64), axis, -1)
    blocks = v.reshape(v.shape[:-1] + (-1, 32))
    amax = np.abs(blocks).max(-1, keepdims=True)
    byte = np.maximum(np.where(amax > 0, np.frexp(amax)[1] - 1 + 127, 0) - down, 1)
    scale = np.exp2(byte - 127.0)
    codes = (blocks / scale).astype(np.float32).astype(dtype).astype(np.float64)
    return np.moveaxis((codes * scale).reshape(v.shape), -1, axis)


WIDE = False


def mx_kscale(k):
    if not WIDE:
        return np.ones(k)
    levels = np.array([10, -10, 5, -5, 0])
    if k % 512:
        return np.exp2(np.random.permutation(np.resize(levels, k // 32))).repeat(32)
    a = np.empty((k // 512, 16))
    for p in range(k // 512):
        a[p, :8] = np.random.permutation(np.resize(levels, 8))
        for g in range(8):
            far = levels[np.abs(levels - a[p, g]) >= 10]
            a[p, g + 8] = far[np.random.randint(len(far))]
    return np.exp2(a.ravel()).repeat(32)


def f64(x):
    return np.asarray(x).astype(np.float64)


def striped(idx):
    return np.tile(idx.reshape(-1, 16).T, (8, 1)).astype(np.uint16)


def unstriped(offs):
    return offs[:16].T.reshape(-1).astype(np.int64)


def pack_weight(w):
    k, n = w.shape
    w = f64(np.asarray(w, np.float32).astype(ml_dtypes.bfloat16)).reshape(k // 32, 32, n)
    amax = np.abs(w).max(1)
    byte = np.clip(np.where(amax > 0, np.frexp(amax)[1] - 1 + 127 - 7, 1), 1, 254)
    scaled = (w * np.exp2(127.0 - byte)[:, None, :]).reshape(k, n).astype(np.float32)
    words = np.ascontiguousarray(scaled.reshape(k // 512, 128, 4, n).transpose(0, 1, 3, 2)).astype(ml_dtypes.float8_e4m3fn).view(np.uint8)
    return words, np.ascontiguousarray(byte.astype(np.uint8).reshape(k // 512, 16, n))


def unpack_weight(words, scales):
    g, p, n, _ = words.shape
    vals = np.ascontiguousarray(words).view(ml_dtypes.float8_e4m3fn).astype(np.float64) * np.repeat(np.exp2(scales.astype(np.float64) - 127.0), 8, axis=1)[..., None]
    return vals.transpose(0, 1, 3, 2).reshape(g * 512, n)


K, T, S, N, H, W, G, U = 512, 2048, 512, 256, 512, 1024, 1024, 1024


def setup_inputs():
    n = np.random.standard_normal
    s = mx_kscale(K)[:, None]
    u = mx_kscale(H)
    packed_xT = pack_weight(n((K, T)) * s)
    packed_eT = pack_weight(n((K, W)) * s)
    packed_dT = pack_weight(n((K, G)) * s)
    return {
        "x_words": packed_xT[0],
        "x_scales": packed_xT[1],
        "w1": (n((K, H)) / np.sqrt(K) / s).astype(np.float32),
        "e_words": packed_eT[0],
        "e_scales": packed_eT[1],
        "w2": (n((K, H)) / np.sqrt(K) / s).astype(np.float32),
        "d_words": packed_dT[0],
        "d_scales": packed_dT[1],
        "w3": (n((K, H)) / np.sqrt(K) / s).astype(np.float32),
        "wa": (np.random.uniform(0.0, 1.0, (H, S))).astype(np.float32),
        "wb": (np.random.uniform(0.0, 1.0, (H, S))).astype(np.float32),
        "unit": (np.random.uniform(0.6, 1.4, (H, 1)) * u[:, None]).astype(np.float32),
        "w4": (n((H, N)) / np.sqrt(H) / u[:, None]).astype(np.float32),
        "offs": striped(np.random.permutation(T)[:S]),
        "bsa": striped(np.random.permutation(W)[:S]),
        "bsb": striped(np.random.permutation(G)[:S]),
        "cor": striped(np.random.permutation(S)),
        "vt": striped(np.random.permutation(np.concatenate([np.arange(S), np.random.randint(0, S, U - S)]))),
    }


def reference(x_words, x_scales, w1, e_words, e_scales, w2, d_words, d_scales, w3, wa, wb, unit, w4, offs, bsa, bsb, cor, vt):
    xq = unpack_weight(x_words, x_scales)[:, unstriped(offs)]
    y = mxq(f64(w1), 0, "e4m3").T @ xq
    e_bsa = unpack_weight(e_words, e_scales)[:, unstriped(bsa)]
    ye = mxq(f64(w2), 0, "e4m3").T @ e_bsa
    d_bsb = unpack_weight(d_words, d_scales)[:, unstriped(bsb)]
    yd = mxq(f64(w3), 0, "e4m3").T @ d_bsb
    bld = y + f64(wa) * ye + f64(wb) * yd
    zc = bld[:, unstriped(cor)]
    corr = (f64(wa) * f64(wb)) * zc
    fix = bld - corr
    fv = fix[:, unstriped(vt)]
    hid = f64(unit) * fv
    return mxq(f64(w4), 0, "e4m3").T @ mxq(hid, 0, "e4m3")

@@ -1,0 +1,262 @@
+from contextlib import ExitStack
+
+import concourse.mybir as mybir
+
+K, T, S, N, H, W, U = 512, 2048, 512, 256, 512, 1024, 1024
+FLOPS = 3 * 2 * K * H * S + 2 * H * N * U
+
+F32 = mybir.dt.float32
+BF16 = mybir.dt.bfloat16
+I32 = mybir.dt.int32
+U32 = mybir.dt.uint32
+U16 = mybir.dt.uint16
+U8 = mybir.dt.uint8
+FP8X4 = mybir.dt.float8_e4m3fn_x4
+MULT = mybir.AluOpType.mult
+ADD = mybir.AluOpType.add
+SUB = mybir.AluOpType.subtract
+COPY = mybir.ActivationFunctionType.Copy
+
+P = 128
+PACK = 4
+PIECE = 256
+LIST_COLS = PIECE // 16
+
+
+def tile_picked_yblshap_cor_p_kernel(
+    tc, x_words, x_scales, w1, e_words, e_scales, w2, d_words, d_scales, w3, wa, wb, unit, w4, offs, bsa, bsb, cor, vt, out
+):
+    nc = tc.nc
+    with ExitStack() as ctx:
+        held = ctx.enter_context(tc.tile_pool(name="held", bufs=1))
+        psum = ctx.enter_context(tc.psum_pool(name="psum", bufs=2))
+
+        def load_list(name, src):
+            tile = held.tile(list(src.shape), U16, name=name)
+            nc.sync.dma_start(tile[:], src)
+            return tile
+
+        def zeroed_plane(name, width):
+            plane = held.tile([P, width], U8, name=name, align_bytes=64)
+            nc.vector.memset(plane[:].bitcast(I32), 0)
+            return plane
+
+        def load_words(name, words):
+            tile = held.tile([P, words.shape[2]], I32, name=name, align_bytes=64)
+            nc.sync.dma_start(tile[:], words[0].rearrange("p n r -> p (n r)").bitcast(I32))
+            return tile
+
+        def load_scales(plane, scales):
+            for q in range(4):
+                nc.sync.dma_start(plane[32 * q : 32 * q + 4, :].bitcast(I32), scales[0, 4 * q : 4 * q + 4, :].bitcast(I32))
+
+        def load_weight(name, w):
+            raw = held.tile([P, PACK, w.shape[1]], F32, name=name)
+            nc.sync.dma_start(raw[:], w.rearrange("(p j) c -> p j c", j=PACK))
+            return raw
+
+        def load_rows(name, w, t):
+            rows = held.tile([P, S], F32, name=name)
+            nc.sync.dma_start(rows[:], w.rearrange("(p t) c -> p t c", t=PACK)[:, t, :])
+            return rows
+
+        def pick_words(name, words, lst):
+            picked = held.tile([P, S], U32, name=name, align_bytes=64)
+            nc.vector.tensor_copy(picked[:], words[:].bitcast(U32).indirect(lst[:]))
+            return picked
+
+        def pick_scales(name, plane, lst):
+            picked = held.tile([P, S], U8, name=name, align_bytes=64)
+            nc.vector.tensor_copy(picked[:], plane[:].indirect(lst[:]))
+            return picked
+
+        def round_dealt(name, raw, t0=0, count=PACK):
+            grouped = held.tile([P, count * H], BF16, name=name, align_bytes=64)
+            nc.scalar.activation(
+                grouped[:].rearrange("p (t m j) -> p m t j", t=count, j=PACK),
+                raw[:].rearrange("p j (m t) -> p m t j", t=PACK)[:, :, t0 : t0 + count, :],
+                COPY,
+            )
+            return grouped
+
+        def quantise(name, grouped, width):
+            codes = held.tile([P, width], U32, name=name + "_codes", align_bytes=64)
+            scales = held.tile([P, width], U8, name=name + "_scales", align_bytes=64)
+            nc.vector.quantize_mx(out=codes[:].bitcast(FP8X4), scales=scales[:], in_=grouped)
+            return codes, scales
+
+        def product(acc, lhs, cols, rhs):
+            nc.tensor.matmul_mx(
+                out=acc,
+                lhsT=lhs[0][:, cols].bitcast(FP8X4),
+                lhsT_scale=lhs[1][:, cols],
+                rhs=rhs[0][:].bitcast(FP8X4),
+                rhs_scale=rhs[1][:],
+                start=True,
+                stop=True,
+            )
+
+        e_plane = zeroed_plane("e_plane", W)
+        d_plane = zeroed_plane("d_plane", W)
+        x_plane = zeroed_plane("x_plane", T)
+
+        wa_rows, wb_rows = {}, {}
+        bsa_list = load_list("bsa_list", bsa)
+        e_tab = load_words("e_tab", e_words)
+        load_scales(e_plane, e_scales)
+        d_tab = load_words("d_tab", d_words)
+        w2_raw = load_weight("w2_raw", w2)
+        bsb_list = load_list("bsb_list", bsb)
+        load_scales(d_plane, d_scales)
+        w3_raw = load_weight("w3_raw", w3)
+        offs_list = load_list("offs_list", offs)
+        x_tab = load_words("x_tab", x_words)
+        load_scales(x_plane, x_scales)
+        w1_raw = load_weight("w1_raw", w1)
+        unit_t = held.tile([P, PACK], F32, name="unit_t")
+        nc.sync.dma_start(unit_t[:], unit.rearrange("(p t) o -> p (t o)", t=PACK))
+        wa_rows[0] = load_rows("wa0", wa, 0)
+        wb_rows[0] = load_rows("wb0", wb, 0)
+        cor_list = load_list("cor_list", cor)
+        wa_rows[1] = load_rows("wa1", wa, 1)
+        wb_rows[1] = load_rows("wb1", wb, 1)
+        vt_list = load_list("vt_list", vt)
+        wa_rows[2] = load_rows("wa2", wa, 2)
+        wb_rows[2] = load_rows("wb2", wb, 2)
+        wa_rows[3] = load_rows("wa3", wa, 3)
+        wb_rows[3] = load_rows("wb3", wb, 3)
+        w4_raw = load_weight("w4_raw", w4)
+
+        term_e, term_d, shapes, both, blend, fixed = {}, {}, {}, {}, {}, {}
+
+        def first_shape(t):
+            ye = psum.tile([P, S], F32, name="ye")
+            product(ye[:], w2_q, slice(t * P, (t + 1) * P), e_picked)
+            term_e[t] = held.tile([P, S], F32, name=f"term_e{t}")
+            nc.vector.scalar_tensor_tensor(term_e[t][:], ye[:], unit_t[:, t : t + 1], wa_rows[t][:], MULT, MULT)
+
+        def second_shape(t):
+            yd = psum.tile([P, S], F32, name="yd")
+            product(yd[:], w3_q, slice(t * P, (t + 1) * P), d_picked)
+            term_d[t] = held.tile([P, S], F32, name=f"term_d{t}")
+            nc.vector.scalar_tensor_tensor(term_d[t][:], yd[:], unit_t[:, t : t + 1], wb_rows[t][:], MULT, MULT)
+
+        def both_weights(t):
+            both[t] = held.tile([P, S], F32, name=f"both{t}")
+            nc.vector.tensor_tensor(both[t][:], wa_rows[t][:], wb_rows[t][:], MULT)
+
+        def sum_shapes(t):
+            shapes[t] = held.tile([P, S], F32, name=f"shapes{t}")
+            nc.vector.tensor_tensor(shapes[t][:], term_e[t][:], term_d[t][:], ADD)
+
+        def blend_rows(t):
+            y = psum.tile([P, S], F32, name="y")
+            product(y[:], w1_q[t // 2], slice(t % 2 * P, (t % 2 + 1) * P), x_picked)
+            blend[t] = held.tile([P, S], F32, name=f"blend{t}")
+            nc.vector.scalar_tensor_tensor(blend[t][:], y[:], unit_t[:, t : t + 1], shapes[t][:], MULT, ADD)
+
+        corr = {}
+
+        def corrective(t):
+            corr[t] = held.tile([P, S], F32, name=f"corr{t}")
+            if t in (3,):
+                for c in range(S // PIECE):
+                    cols = slice(c * PIECE, (c + 1) * PIECE)
+                    picked = blend[t][:].indirect(cor_list[:, c * LIST_COLS : (c + 1) * LIST_COLS])
+                    nc.vector.tensor_tensor(corr[t][:, cols], picked, both[t][:, cols], MULT)
+            else:
+                other = held.tile([P, S], F32, name=f"other{t}")
+                for c in range(S // PIECE):
+                    cols = slice(c * PIECE, (c + 1) * PIECE)
+                    picked = blend[t][:].indirect(cor_list[:, c * LIST_COLS : (c + 1) * LIST_COLS])
+                    nc.scalar.activation(other[:, cols], picked, COPY)
+                nc.vector.tensor_tensor(corr[t][:], other[:], both[t][:], MULT)
+
+        planes = [held.tile([P, PACK, PIECE], BF16, name=f"planes{c}", align_bytes=64) for c in range(U // PIECE)]
+
+        def fix_rows(t):
+            fixed[t] = held.tile([P, S], F32, name=f"fixed{t}")
+            nc.vector.tensor_tensor(fixed[t][:], blend[t][:], corr[t][:], SUB)
+
+        def look_up(t, c):
+            picked = fixed[t][:].indirect(vt_list[:, c * LIST_COLS : (c + 1) * LIST_COLS])
+            nc.scalar.activation(planes[c][:, t, :], picked, COPY)
+
+        e_picked = (pick_words("e_pw", e_tab, bsa_list), pick_scales("e_ps", e_plane, bsa_list))
+        d_picked = (pick_words("d_pw", d_tab, bsb_list), pick_scales("d_ps", d_plane, bsb_list))
+        w2_q = quantise("w2", round_dealt("w2_bf", w2_raw)[:], H)
+        x_picked = (pick_words("x_pw", x_tab, offs_list), pick_scales("x_ps", x_plane, offs_list))
+        w3_q = quantise("w3", round_dealt("w3_bf", w3_raw)[:], H)
+        first_shape(0)
+        second_shape(0)
+        w1_q = [quantise("w1a", round_dealt("w1a_bf", w1_raw, 0, 2)[:], H // 2)]
+        sum_shapes(0)
+        both_weights(0)
+        blend_rows(0)
+        first_shape(1)
+        w1_q.append(quantise("w1b", round_dealt("w1b_bf", w1_raw, 2, 2)[:], H // 2))
+        second_shape(1)
+        both_weights(1)
+        sum_shapes(1)
+        corrective(0)
+        blend_rows(1)
+        fix_rows(0)
+        first_shape(2)
+        second_shape(2)
+        both_weights(2)
+        corrective(1)
+        for c in range(4):
+            look_up(0, c)
+        sum_shapes(2)
+        fix_rows(1)
+        blend_rows(2)
+        look_up(1, 0)
+        first_shape(3)
+        second_shape(3)
+        corrective(2)
+        look_up(1, 1)
+        look_up(1, 2)
+        look_up(1, 3)
+        both_weights(3)
+        fix_rows(2)
+        sum_shapes(3)
+        for c in range(4):
+            look_up(2, c)
+        w4_bf = held.tile([P, N, PACK], BF16, name="w4_bf", align_bytes=64)
+        nc.scalar.activation(w4_bf[:], w4_raw[:].rearrange("p j c -> p c j"), COPY)
+        w4_q = quantise("w4", w4_bf[:].rearrange("p c j -> p (c j)"), N)
+        blend_rows(3)
+        corrective(3)
+        fix_rows(3)
+        for c in range(4):
+            look_up(3, c)
+
+
+        out_rows = out.rearrange("(h p) r -> p h r", p=P)
+        hid_bf = {}
+
+        def weave(c):
+            hid_bf[c] = held.tile([P, PIECE, PACK], BF16, name=f"hid_bf{c}", align_bytes=64)
+            src = planes[c][:].rearrange("p t r -> p r t")
+            if c in ():
+                nc.scalar.copy(hid_bf[c][:], src)
+            else:
+                nc.vector.tensor_copy(hid_bf[c][:], src)
+
+        def decode(c):
+            hid_q = quantise(f"hid{c}", hid_bf[c][:].rearrange("p r t -> p (r t)"), PIECE)
+            acc = psum.tile([P, N // P, PIECE], F32, name="acc")
+            for h in range(N // P):
+                product(acc[:, h, :], w4_q, slice(h * P, (h + 1) * P), hid_q)
+            result = held.tile([P, N // P, PIECE], F32, name=f"result{c}")
+            if c in ():
+                nc.vector.tensor_copy(result[:], acc[:])
+            else:
+                nc.scalar.copy(result[:], acc[:])
+            nc.sync.dma_start(out_rows[:, :, c * PIECE : (c + 1) * PIECE], result[:])
+
+        weave(0)
+        for c in range(1, U // PIECE):
+            weave(c)
+            decode(c - 1)
+        decode(U // PIECE - 1)

@@ -46,9 +46,9 @@ def tile_picked_yblshap_cor_p_kernel(
             nc.sync.dma_start(tile[:], words[0].rearrange("p n r -> p (n r)").bitcast(I32))
             return tile
 
-        def load_scales(plane, scales):
+        def load_scales(plane, scales, row):
             for q in range(4):
-                nc.sync.dma_start(plane[32 * q : 32 * q + 4, :].bitcast(I32), scales[0, 4 * q : 4 * q + 4, :].bitcast(I32))
+                nc.sync.dma_start(plane[32 * q + row : 32 * q + row + 4, :].bitcast(I32), scales[0, 4 * q : 4 * q + 4, :].bitcast(I32))
 
         def load_weight(name, w):
             raw = held.tile([P, PACK, w.shape[1]], F32, name=name)
@@ -73,8 +73,8 @@ def tile_picked_yblshap_cor_p_kernel(
         def round_dealt(name, raw, t0=0, count=PACK):
             grouped = held.tile([P, count * H], BF16, name=name, align_bytes=64)
             nc.scalar.activation(
-                grouped[:].rearrange("p (t m j) -> p m t j", t=count, j=PACK),
-                raw[:].rearrange("p j (m t) -> p m t j", t=PACK)[:, :, t0 : t0 + count, :],
+                grouped[:].rearrange("p (t m j) -> p m j t", t=count, j=PACK),
+                raw[:].rearrange("p j (m t) -> p m j t", t=PACK)[:, :, :, t0 : t0 + count],
                 COPY,
             )
             return grouped
@@ -85,13 +85,13 @@ def tile_picked_yblshap_cor_p_kernel(
             nc.vector.quantize_mx(out=codes[:].bitcast(FP8X4), scales=scales[:], in_=grouped)
             return codes, scales
 
-        def product(acc, lhs, cols, rhs):
+        def product(acc, lhs, cols, rhs, row=0):
             nc.tensor.matmul_mx(
                 out=acc,
                 lhsT=lhs[0][:, cols].bitcast(FP8X4),
                 lhsT_scale=lhs[1][:, cols],
                 rhs=rhs[0][:].bitcast(FP8X4),
-                rhs_scale=rhs[1][:],
+                rhs_scale=rhs[1][row:P, :],
                 start=True,
                 stop=True,
             )
@@ -103,20 +103,20 @@ def tile_picked_yblshap_cor_p_kernel(
         wa_rows, wb_rows = {}, {}
         bsa_list = load_list("bsa_list", bsa)
         e_tab = load_words("e_tab", e_words)
-        load_scales(e_plane, e_scales)
-        d_tab = load_words("d_tab", d_words)
+        load_scales(e_plane, e_scales, 0)
         w2_raw = load_weight("w2_raw", w2)
+        d_tab = load_words("d_tab", d_words)
         bsb_list = load_list("bsb_list", bsb)
-        load_scales(d_plane, d_scales)
+        load_scales(d_plane, d_scales, 4)
         w3_raw = load_weight("w3_raw", w3)
-        offs_list = load_list("offs_list", offs)
-        x_tab = load_words("x_tab", x_words)
-        load_scales(x_plane, x_scales)
-        w1_raw = load_weight("w1_raw", w1)
         unit_t = held.tile([P, PACK], F32, name="unit_t")
         nc.sync.dma_start(unit_t[:], unit.rearrange("(p t) o -> p (t o)", t=PACK))
         wa_rows[0] = load_rows("wa0", wa, 0)
         wb_rows[0] = load_rows("wb0", wb, 0)
+        offs_list = load_list("offs_list", offs)
+        x_tab = load_words("x_tab", x_words)
+        load_scales(x_plane, x_scales, 8)
+        w1_raw = load_weight("w1_raw", w1)
         cor_list = load_list("cor_list", cor)
         wa_rows[1] = load_rows("wa1", wa, 1)
         wb_rows[1] = load_rows("wb1", wb, 1)
@@ -137,7 +137,7 @@ def tile_picked_yblshap_cor_p_kernel(
 
         def second_shape(t):
             yd = psum.tile([P, S], F32, name="yd")
-            product(yd[:], w3_q, slice(t * P, (t + 1) * P), d_picked)
+            product(yd[:], w3_q, slice(t * P, (t + 1) * P), d_picked, 4)
             term_d[t] = held.tile([P, S], F32, name=f"term_d{t}")
             nc.vector.scalar_tensor_tensor(term_d[t][:], yd[:], unit_t[:, t : t + 1], wb_rows[t][:], MULT, MULT)
 
@@ -151,7 +151,7 @@ def tile_picked_yblshap_cor_p_kernel(
 
         def blend_rows(t):
             y = psum.tile([P, S], F32, name="y")
-            product(y[:], w1_q[t // 2], slice(t % 2 * P, (t % 2 + 1) * P), x_picked)
+            product(y[:], w1_q[t // 2], slice(t % 2 * P, (t % 2 + 1) * P), x_picked, 8)
             blend[t] = held.tile([P, S], F32, name=f"blend{t}")
             nc.vector.scalar_tensor_tensor(blend[t][:], y[:], unit_t[:, t : t + 1], shapes[t][:], MULT, ADD)
 
@@ -185,47 +185,47 @@ def tile_picked_yblshap_cor_p_kernel(
         e_picked = (pick_words("e_pw", e_tab, bsa_list), pick_scales("e_ps", e_plane, bsa_list))
         d_picked = (pick_words("d_pw", d_tab, bsb_list), pick_scales("d_ps", d_plane, bsb_list))
         w2_q = quantise("w2", round_dealt("w2_bf", w2_raw)[:], H)
-        x_picked = (pick_words("x_pw", x_tab, offs_list), pick_scales("x_ps", x_plane, offs_list))
-        w3_q = quantise("w3", round_dealt("w3_bf", w3_raw)[:], H)
-        first_shape(0)
-        second_shape(0)
-        w1_q = [quantise("w1a", round_dealt("w1a_bf", w1_raw, 0, 2)[:], H // 2)]
-        sum_shapes(0)
         both_weights(0)
-        blend_rows(0)
+        first_shape(0)
+        w3_q = quantise("w3", round_dealt("w3_bf", w3_raw)[:], H)
+        x_picked = (pick_words("x_pw", x_tab, offs_list), pick_scales("x_ps", x_plane, offs_list))
+        second_shape(0)
         first_shape(1)
-        w1_q.append(quantise("w1b", round_dealt("w1b_bf", w1_raw, 2, 2)[:], H // 2))
+        sum_shapes(0)
+        w1_q = [quantise("w1a", round_dealt("w1a_bf", w1_raw, 0, 2)[:], H // 2)]
         second_shape(1)
         both_weights(1)
+        blend_rows(0)
+        w1_q.append(quantise("w1b", round_dealt("w1b_bf", w1_raw, 2, 2)[:], H // 2))
         sum_shapes(1)
         corrective(0)
         blend_rows(1)
-        fix_rows(0)
         first_shape(2)
         second_shape(2)
+        fix_rows(0)
         both_weights(2)
+        sum_shapes(2)
         corrective(1)
         for c in range(4):
             look_up(0, c)
-        sum_shapes(2)
-        fix_rows(1)
         blend_rows(2)
-        look_up(1, 0)
         first_shape(3)
         second_shape(3)
-        corrective(2)
-        look_up(1, 1)
-        look_up(1, 2)
-        look_up(1, 3)
+        fix_rows(1)
+        w4_bf = held.tile([P, N, PACK], BF16, name="w4_bf", align_bytes=64)
+        nc.scalar.activation(
+            w4_bf[:].rearrange("p (c i) j -> p c j i", i=4), w4_raw[:].rearrange("p j (c i) -> p c j i", i=4), COPY
+        )
+        w4_q = quantise("w4", w4_bf[:].rearrange("p c j -> p (c j)"), N)
         both_weights(3)
-        fix_rows(2)
         sum_shapes(3)
+        corrective(2)
+        for c in range(4):
+            look_up(1, c)
+        blend_rows(3)
+        fix_rows(2)
         for c in range(4):
             look_up(2, c)
-        w4_bf = held.tile([P, N, PACK], BF16, name="w4_bf", align_bytes=64)
-        nc.scalar.activation(w4_bf[:], w4_raw[:].rearrange("p j c -> p c j"), COPY)
-        w4_q = quantise("w4", w4_bf[:].rearrange("p c j -> p (c j)"), N)
-        blend_rows(3)
         corrective(3)
         fix_rows(3)
         for c in range(4):
@@ -237,26 +237,42 @@ def tile_picked_yblshap_cor_p_kernel(
 
         def weave(c):
             hid_bf[c] = held.tile([P, PIECE, PACK], BF16, name=f"hid_bf{c}", align_bytes=64)
-            src = planes[c][:].rearrange("p t r -> p r t")
-            if c in ():
-                nc.scalar.copy(hid_bf[c][:], src)
+            src = planes[c][:].rearrange("p t (r i) -> p r t i", i=4)
+            dst = hid_bf[c][:].rearrange("p (r i) t -> p r t i", i=4)
+            if c in (3,):
+                nc.scalar.copy(dst, src)
             else:
-                nc.vector.tensor_copy(hid_bf[c][:], src)
+                nc.vector.tensor_copy(dst, src)
+
+        hid_q, acc = {}, {}
+        last = U // PIECE - 1
+
+        def quantise_hid(c):
+            hid_q[c] = quantise(f"hid{c}", hid_bf[c][:].rearrange("p r t -> p (r t)"), PIECE)
 
         def decode(c):
-            hid_q = quantise(f"hid{c}", hid_bf[c][:].rearrange("p r t -> p (r t)"), PIECE)
-            acc = psum.tile([P, N // P, PIECE], F32, name="acc")
+            acc = psum.tile([P, N // P, PIECE], F32, name=("acc", "acc", "ye")[c])
             for h in range(N // P):
-                product(acc[:, h, :], w4_q, slice(h * P, (h + 1) * P), hid_q)
+                product(acc[:, h, :], w4_q, slice(h * P, (h + 1) * P), hid_q[c])
             result = held.tile([P, N // P, PIECE], F32, name=f"result{c}")
-            if c in ():
-                nc.vector.tensor_copy(result[:], acc[:])
-            else:
-                nc.scalar.copy(result[:], acc[:])
+            nc.scalar.copy(result[:], acc[:])
             nc.sync.dma_start(out_rows[:, :, c * PIECE : (c + 1) * PIECE], result[:])
 
+        def decode_last(c):
+            for h, copy in enumerate((nc.scalar.copy, nc.vector.tensor_copy)):
+                acc = psum.tile([P, PIECE], F32, name=("yd", "y")[h])
+                product(acc[:], w4_q, slice(h * P, (h + 1) * P), hid_q[c])
+                result = held.tile([P, PIECE], F32, name=f"result{c}_{h}")
+                copy(result[:], acc[:])
+                nc.sync.dma_start(out_rows[:, h, c * PIECE : (c + 1) * PIECE], result[:])
+
+        weave(last)
         weave(0)
-        for c in range(1, U // PIECE):
+        for c in range(1, last):
             weave(c)
-            decode(c - 1)
-        decode(U // PIECE - 1)
+            quantise_hid(c - 1)
+        quantise_hid(last - 1)
+        quantise_hid(last)
+        for c in range(last):
+            decode(c)
+        decode_last(last)

@@ -2,7 +2,7 @@ from contextlib import ExitStack
 
 import concourse.mybir as mybir
 
-K, T, S, N, H, W, U = 512, 2048, 512, 256, 512, 1024, 1024
+K, H, S, U, N = 512, 512, 512, 1024, 256
 FLOPS = 3 * 2 * K * H * S + 2 * H * N * U
 
 F32 = mybir.dt.float32
@@ -19,8 +19,14 @@ COPY = mybir.ActivationFunctionType.Copy
 
 P = 128
 PACK = 4
-PIECE = 256
-LIST_COLS = PIECE // 16
+LAST_TILE = PACK - 1
+QUADRANT = 32
+PER_COLUMN = 16
+RUN = 4
+CHUNK = 256
+CHUNKS = U // CHUNK
+LAST_CHUNK = CHUNKS - 1
+E_FIRST, D_FIRST, X_FIRST = 0, 4, 8
 
 
 def tile_picked_yblshap_cor_p_kernel(
@@ -31,248 +37,241 @@ def tile_picked_yblshap_cor_p_kernel(
         held = ctx.enter_context(tc.tile_pool(name="held", bufs=1))
         psum = ctx.enter_context(tc.psum_pool(name="psum", bufs=2))
 
+
         def load_list(name, src):
             tile = held.tile(list(src.shape), U16, name=name)
             nc.sync.dma_start(tile[:], src)
             return tile
-
-        def zeroed_plane(name, width):
-            plane = held.tile([P, width], U8, name=name, align_bytes=64)
-            nc.vector.memset(plane[:].bitcast(I32), 0)
-            return plane
 
         def load_words(name, words):
             tile = held.tile([P, words.shape[2]], I32, name=name, align_bytes=64)
             nc.sync.dma_start(tile[:], words[0].rearrange("p n r -> p (n r)").bitcast(I32))
             return tile
 
-        def load_scales(plane, scales, row):
-            for q in range(4):
-                nc.sync.dma_start(plane[32 * q + row : 32 * q + row + 4, :].bitcast(I32), scales[0, 4 * q : 4 * q + 4, :].bitcast(I32))
+        def zeroed_scale_tile(name, scales):
+            tile = held.tile([P, scales.shape[2]], U8, name=name, align_bytes=64)
+            nc.vector.memset(tile[:].bitcast(I32), 0)
+            return tile
+
+        def load_scales(tile, scales, first):
+            for q in range(P // QUADRANT):
+                p0 = QUADRANT * q + first
+                nc.sync.dma_start(tile[p0 : p0 + 4, :].bitcast(I32), scales[0, 4 * q : 4 * q + 4, :].bitcast(I32))
 
         def load_weight(name, w):
             raw = held.tile([P, PACK, w.shape[1]], F32, name=name)
             nc.sync.dma_start(raw[:], w.rearrange("(p j) c -> p j c", j=PACK))
             return raw
 
-        def load_rows(name, w, t):
-            rows = held.tile([P, S], F32, name=name)
-            nc.sync.dma_start(rows[:], w.rearrange("(p t) c -> p t c", t=PACK)[:, t, :])
-            return rows
+        def load_row_tiles(name, w, t0, count):
+            rows = held.tile([P, count, S], F32, name=f"{name}{t0}")
+            nc.sync.dma_start(rows[:], w.rearrange("(p t) c -> p t c", t=PACK)[:, t0 : t0 + count, :])
+            return [rows[:, t, :] for t in range(count)]
 
-        def pick_words(name, words, lst):
-            picked = held.tile([P, S], U32, name=name, align_bytes=64)
-            nc.vector.tensor_copy(picked[:], words[:].bitcast(U32).indirect(lst[:]))
-            return picked
+        e_scale_tile = zeroed_scale_tile("e_scale_tile", e_scales)
+        d_scale_tile = zeroed_scale_tile("d_scale_tile", d_scales)
+        x_scale_tile = zeroed_scale_tile("x_scale_tile", x_scales)
 
-        def pick_scales(name, plane, lst):
-            picked = held.tile([P, S], U8, name=name, align_bytes=64)
-            nc.vector.tensor_copy(picked[:], plane[:].indirect(lst[:]))
-            return picked
+        bsa_list = load_list("bsa_list", bsa)
+        e_word_tile = load_words("e_word_tile", e_words)
+        load_scales(e_scale_tile, e_scales, E_FIRST)
+        w2_raw = load_weight("w2_raw", w2)
+        d_word_tile = load_words("d_word_tile", d_words)
+        bsb_list = load_list("bsb_list", bsb)
+        load_scales(d_scale_tile, d_scales, D_FIRST)
+        w3_raw = load_weight("w3_raw", w3)
+        unit_rows = held.tile([P, PACK], F32, name="unit_rows")
+        nc.sync.dma_start(unit_rows[:], unit.rearrange("(p t) o -> p (t o)", t=PACK))
+        wa_rows = load_row_tiles("wa", wa, 0, 1)
+        wb_rows = load_row_tiles("wb", wb, 0, 1)
+        offs_list = load_list("offs_list", offs)
+        x_word_tile = load_words("x_word_tile", x_words)
+        load_scales(x_scale_tile, x_scales, X_FIRST)
+        w1_raw = load_weight("w1_raw", w1)
+        cor_list = load_list("cor_list", cor)
+        wa_rows.extend(load_row_tiles("wa", wa, 1, 1))
+        wb_rows.extend(load_row_tiles("wb", wb, 1, 1))
+        vt_list = load_list("vt_list", vt)
+        wa_rows.extend(load_row_tiles("wa", wa, 2, 1))
+        wb_rows.extend(load_row_tiles("wb", wb, 2, 1))
+        wa_rows.extend(load_row_tiles("wa", wa, 3, 1))
+        wb_rows.extend(load_row_tiles("wb", wb, 3, 1))
+        w4_raw = load_weight("w4_raw", w4)
 
-        def round_dealt(name, raw, t0=0, count=PACK):
-            grouped = held.tile([P, count * H], BF16, name=name, align_bytes=64)
+
+        def pick(name, word_tile, scale_tile, first, offsets):
+            words = held.tile([P, S], U32, name=name + "_words", align_bytes=64)
+            nc.vector.tensor_copy(words[:], word_tile[:].bitcast(U32).indirect(offsets[:]))
+            scales = held.tile([P, S], U8, name=name + "_scales", align_bytes=64)
+            nc.vector.tensor_copy(scales[:], scale_tile[:].indirect(offsets[:]))
+            return words[:], scales[first:P, :]
+
+        def quantise(name, grouped):
+            width = grouped.shape[1] // PACK
+            words = held.tile([P, width], U32, name=name + "_words", align_bytes=64)
+            scales = held.tile([P, width], U8, name=name + "_scales", align_bytes=64)
+            nc.vector.quantize_mx(out=words[:].bitcast(FP8X4), scales=scales[:], in_=grouped)
+            return words[:], scales[:]
+
+        def quantise_dealt(name, raw, t0, count):
+            grouped = held.tile([P, count * P * PACK], BF16, name=f"{name}_bf{t0}", align_bytes=64)
             nc.scalar.activation(
                 grouped[:].rearrange("p (t m j) -> p m j t", t=count, j=PACK),
                 raw[:].rearrange("p j (m t) -> p m j t", t=PACK)[:, :, :, t0 : t0 + count],
                 COPY,
             )
-            return grouped
+            return split_stationary(quantise(f"{name}_{t0}", grouped[:]))
 
-        def quantise(name, grouped, width):
-            codes = held.tile([P, width], U32, name=name + "_codes", align_bytes=64)
-            scales = held.tile([P, width], U8, name=name + "_scales", align_bytes=64)
-            nc.vector.quantize_mx(out=codes[:].bitcast(FP8X4), scales=scales[:], in_=grouped)
-            return codes, scales
+        def split_stationary(operand):
+            words, scales = operand
+            return [(words[:, c : c + P], scales[:, c : c + P]) for c in range(0, words.shape[1], P)]
 
-        def product(acc, lhs, cols, rhs, row=0):
+        def product(acc, stationary, moving):
             nc.tensor.matmul_mx(
                 out=acc,
-                lhsT=lhs[0][:, cols].bitcast(FP8X4),
-                lhsT_scale=lhs[1][:, cols],
-                rhs=rhs[0][:].bitcast(FP8X4),
-                rhs_scale=rhs[1][row:P, :],
+                lhsT=stationary[0].bitcast(FP8X4),
+                lhsT_scale=stationary[1],
+                rhs=moving[0].bitcast(FP8X4),
+                rhs_scale=moving[1],
                 start=True,
                 stop=True,
             )
 
-        e_plane = zeroed_plane("e_plane", W)
-        d_plane = zeroed_plane("d_plane", W)
-        x_plane = zeroed_plane("x_plane", T)
+        term_e, term_d, both, blend_tile, fixed_tile = {}, {}, {}, {}, {}
 
-        wa_rows, wb_rows = {}, {}
-        bsa_list = load_list("bsa_list", bsa)
-        e_tab = load_words("e_tab", e_words)
-        load_scales(e_plane, e_scales, 0)
-        w2_raw = load_weight("w2_raw", w2)
-        d_tab = load_words("d_tab", d_words)
-        bsb_list = load_list("bsb_list", bsb)
-        load_scales(d_plane, d_scales, 4)
-        w3_raw = load_weight("w3_raw", w3)
-        unit_t = held.tile([P, PACK], F32, name="unit_t")
-        nc.sync.dma_start(unit_t[:], unit.rearrange("(p t) o -> p (t o)", t=PACK))
-        wa_rows[0] = load_rows("wa0", wa, 0)
-        wb_rows[0] = load_rows("wb0", wb, 0)
-        offs_list = load_list("offs_list", offs)
-        x_tab = load_words("x_tab", x_words)
-        load_scales(x_plane, x_scales, 8)
-        w1_raw = load_weight("w1_raw", w1)
-        cor_list = load_list("cor_list", cor)
-        wa_rows[1] = load_rows("wa1", wa, 1)
-        wb_rows[1] = load_rows("wb1", wb, 1)
-        vt_list = load_list("vt_list", vt)
-        wa_rows[2] = load_rows("wa2", wa, 2)
-        wb_rows[2] = load_rows("wb2", wb, 2)
-        wa_rows[3] = load_rows("wa3", wa, 3)
-        wb_rows[3] = load_rows("wb3", wb, 3)
-        w4_raw = load_weight("w4_raw", w4)
-
-        term_e, term_d, shapes, both, blend, fixed = {}, {}, {}, {}, {}, {}
+        def weighted_product(tag, stationary, moving, t, result, other, op):
+            acc = psum.tile([P, S], F32, name=tag)
+            product(acc[:], stationary, moving)
+            nc.vector.scalar_tensor_tensor(result, acc[:], unit_rows[:, t : t + 1], other, MULT, op)
 
         def first_shape(t):
-            ye = psum.tile([P, S], F32, name="ye")
-            product(ye[:], w2_q, slice(t * P, (t + 1) * P), e_picked)
             term_e[t] = held.tile([P, S], F32, name=f"term_e{t}")
-            nc.vector.scalar_tensor_tensor(term_e[t][:], ye[:], unit_t[:, t : t + 1], wa_rows[t][:], MULT, MULT)
+            weighted_product("ye", w2_q[t], e_picked, t, term_e[t][:], wa_rows[t], MULT)
 
         def second_shape(t):
-            yd = psum.tile([P, S], F32, name="yd")
-            product(yd[:], w3_q, slice(t * P, (t + 1) * P), d_picked, 4)
             term_d[t] = held.tile([P, S], F32, name=f"term_d{t}")
-            nc.vector.scalar_tensor_tensor(term_d[t][:], yd[:], unit_t[:, t : t + 1], wb_rows[t][:], MULT, MULT)
+            weighted_product("yd", w3_q[t], d_picked, t, term_d[t][:], wb_rows[t], MULT)
 
         def both_weights(t):
             both[t] = held.tile([P, S], F32, name=f"both{t}")
-            nc.vector.tensor_tensor(both[t][:], wa_rows[t][:], wb_rows[t][:], MULT)
+            nc.vector.tensor_tensor(both[t][:], wa_rows[t], wb_rows[t], MULT)
 
         def sum_shapes(t):
-            shapes[t] = held.tile([P, S], F32, name=f"shapes{t}")
-            nc.vector.tensor_tensor(shapes[t][:], term_e[t][:], term_d[t][:], ADD)
+            blend_tile[t] = held.tile([P, 2 * S], F32, name=f"blend{t}")
+            nc.vector.tensor_tensor(blend_tile[t][:, S:], term_e[t][:], term_d[t][:], ADD)
 
-        def blend_rows(t):
-            y = psum.tile([P, S], F32, name="y")
-            product(y[:], w1_q[t // 2], slice(t % 2 * P, (t % 2 + 1) * P), x_picked, 8)
-            blend[t] = held.tile([P, S], F32, name=f"blend{t}")
-            nc.vector.scalar_tensor_tensor(blend[t][:], y[:], unit_t[:, t : t + 1], shapes[t][:], MULT, ADD)
-
-        corr = {}
+        def blend(t):
+            weighted_product("y", w1_q[t], x_picked, t, blend_tile[t][:, :S], blend_tile[t][:, S:], ADD)
 
         def corrective(t):
-            corr[t] = held.tile([P, S], F32, name=f"corr{t}")
-            if t in (3,):
-                for c in range(S // PIECE):
-                    cols = slice(c * PIECE, (c + 1) * PIECE)
-                    picked = blend[t][:].indirect(cor_list[:, c * LIST_COLS : (c + 1) * LIST_COLS])
-                    nc.vector.tensor_tensor(corr[t][:, cols], picked, both[t][:, cols], MULT)
-            else:
-                other = held.tile([P, S], F32, name=f"other{t}")
-                for c in range(S // PIECE):
-                    cols = slice(c * PIECE, (c + 1) * PIECE)
-                    picked = blend[t][:].indirect(cor_list[:, c * LIST_COLS : (c + 1) * LIST_COLS])
-                    nc.scalar.activation(other[:, cols], picked, COPY)
-                nc.vector.tensor_tensor(corr[t][:], other[:], both[t][:], MULT)
+            fixed_tile[t] = held.tile([P, 2 * S], F32, name=f"fixed{t}")
+            other_vertex = blend_tile[t][:].indirect(cor_list[:])
+            if t != LAST_TILE:
+                fetched = held.tile([P, S], F32, name=f"fetched{t}")
+                nc.scalar.activation(fetched[:], other_vertex, COPY)
+                other_vertex = fetched[:]
+            nc.vector.tensor_tensor(fixed_tile[t][:, S:], other_vertex, both[t][:], MULT)
 
-        planes = [held.tile([P, PACK, PIECE], BF16, name=f"planes{c}", align_bytes=64) for c in range(U // PIECE)]
+        def fix(t):
+            nc.vector.tensor_tensor(fixed_tile[t][:, :S], blend_tile[t][:, :S], fixed_tile[t][:, S:], SUB)
 
-        def fix_rows(t):
-            fixed[t] = held.tile([P, S], F32, name=f"fixed{t}")
-            nc.vector.tensor_tensor(fixed[t][:], blend[t][:], corr[t][:], SUB)
+        hid_rows = [held.tile([P, PACK, U // 2], BF16, name=f"hid_rows{half}", align_bytes=64) for half in range(2)]
 
-        def look_up(t, c):
-            picked = fixed[t][:].indirect(vt_list[:, c * LIST_COLS : (c + 1) * LIST_COLS])
-            nc.scalar.activation(planes[c][:, t, :], picked, COPY)
+        def look_up(t):
+            width = CHUNK if t == LAST_TILE else U // 2
+            for r0 in range(0, U, width):
+                corners = fixed_tile[t][:].indirect(vt_list[:, r0 // PER_COLUMN : (r0 + width) // PER_COLUMN])
+                half, c0 = divmod(r0, U // 2)
+                nc.scalar.activation(hid_rows[half][:, t, c0 : c0 + width], corners, COPY)
 
-        e_picked = (pick_words("e_pw", e_tab, bsa_list), pick_scales("e_ps", e_plane, bsa_list))
-        d_picked = (pick_words("d_pw", d_tab, bsb_list), pick_scales("d_ps", d_plane, bsb_list))
-        w2_q = quantise("w2", round_dealt("w2_bf", w2_raw)[:], H)
+        def quantise_w4():
+            grouped = held.tile([P, N, PACK], BF16, name="w4_bf", align_bytes=64)
+            nc.scalar.activation(
+                grouped[:].rearrange("p (c i) j -> p c j i", i=RUN),
+                w4_raw[:].rearrange("p j (c i) -> p c j i", i=RUN),
+                COPY,
+            )
+            return split_stationary(quantise("w4", grouped[:].rearrange("p c j -> p (c j)")))
+
+        e_picked = pick("e_picked", e_word_tile, e_scale_tile, E_FIRST, bsa_list)
+        d_picked = pick("d_picked", d_word_tile, d_scale_tile, D_FIRST, bsb_list)
+        w2_q = quantise_dealt("w2", w2_raw, 0, PACK)
         both_weights(0)
         first_shape(0)
-        w3_q = quantise("w3", round_dealt("w3_bf", w3_raw)[:], H)
-        x_picked = (pick_words("x_pw", x_tab, offs_list), pick_scales("x_ps", x_plane, offs_list))
+        w3_q = quantise_dealt("w3", w3_raw, 0, PACK)
+        x_picked = pick("x_picked", x_word_tile, x_scale_tile, X_FIRST, offs_list)
         second_shape(0)
         first_shape(1)
         sum_shapes(0)
-        w1_q = [quantise("w1a", round_dealt("w1a_bf", w1_raw, 0, 2)[:], H // 2)]
+        w1_q = quantise_dealt("w1", w1_raw, 0, 2)
         second_shape(1)
         both_weights(1)
-        blend_rows(0)
-        w1_q.append(quantise("w1b", round_dealt("w1b_bf", w1_raw, 2, 2)[:], H // 2))
+        blend(0)
+        w1_q.extend(quantise_dealt("w1", w1_raw, 2, 2))
         sum_shapes(1)
         corrective(0)
-        blend_rows(1)
+        blend(1)
         first_shape(2)
         second_shape(2)
-        fix_rows(0)
+        fix(0)
         both_weights(2)
         sum_shapes(2)
         corrective(1)
-        for c in range(4):
-            look_up(0, c)
-        blend_rows(2)
+        look_up(0)
+        blend(2)
         first_shape(3)
+        fix(1)
+        w4_q = quantise_w4()
         second_shape(3)
-        fix_rows(1)
-        w4_bf = held.tile([P, N, PACK], BF16, name="w4_bf", align_bytes=64)
-        nc.scalar.activation(
-            w4_bf[:].rearrange("p (c i) j -> p c j i", i=4), w4_raw[:].rearrange("p j (c i) -> p c j i", i=4), COPY
-        )
-        w4_q = quantise("w4", w4_bf[:].rearrange("p c j -> p (c j)"), N)
-        both_weights(3)
-        sum_shapes(3)
         corrective(2)
-        for c in range(4):
-            look_up(1, c)
-        blend_rows(3)
-        fix_rows(2)
-        for c in range(4):
-            look_up(2, c)
+        look_up(1)
+        sum_shapes(3)
+        fix(2)
+        look_up(2)
+        both_weights(3)
+        blend(3)
         corrective(3)
-        fix_rows(3)
-        for c in range(4):
-            look_up(3, c)
-
+        fix(3)
+        look_up(3)
 
         out_rows = out.rearrange("(h p) r -> p h r", p=P)
-        hid_bf = {}
+        hid_grouped, hid_q = {}, {}
 
-        def weave(c):
-            hid_bf[c] = held.tile([P, PIECE, PACK], BF16, name=f"hid_bf{c}", align_bytes=64)
-            src = planes[c][:].rearrange("p t (r i) -> p r t i", i=4)
-            dst = hid_bf[c][:].rearrange("p (r i) t -> p r t i", i=4)
-            if c in (3,):
-                nc.scalar.copy(dst, src)
-            else:
-                nc.vector.tensor_copy(dst, src)
-
-        hid_q, acc = {}, {}
-        last = U // PIECE - 1
+        def interleave(c):
+            half, c0 = divmod(c * CHUNK, U // 2)
+            hid_grouped[c] = held.tile([P, CHUNK, PACK], BF16, name=f"hid_grouped{c}", align_bytes=64)
+            copy = nc.scalar.copy if c == LAST_CHUNK else nc.vector.tensor_copy
+            copy(
+                hid_grouped[c][:].rearrange("p (r i) t -> p r t i", i=RUN),
+                hid_rows[half][:, :, c0 : c0 + CHUNK].rearrange("p t (r i) -> p r t i", i=RUN),
+            )
 
         def quantise_hid(c):
-            hid_q[c] = quantise(f"hid{c}", hid_bf[c][:].rearrange("p r t -> p (r t)"), PIECE)
+            hid_q[c] = quantise(f"hid{c}", hid_grouped[c][:].rearrange("p r t -> p (r t)"))
 
-        def decode(c):
-            acc = psum.tile([P, N // P, PIECE], F32, name=("acc", "acc", "ye")[c])
+        def decode(c, tag):
+            acc = psum.tile([P, N // P, CHUNK], F32, name=tag)
             for h in range(N // P):
-                product(acc[:, h, :], w4_q, slice(h * P, (h + 1) * P), hid_q[c])
-            result = held.tile([P, N // P, PIECE], F32, name=f"result{c}")
+                product(acc[:, h, :], w4_q[h], hid_q[c])
+            result = held.tile([P, N // P, CHUNK], F32, name=f"result{c}")
             nc.scalar.copy(result[:], acc[:])
-            nc.sync.dma_start(out_rows[:, :, c * PIECE : (c + 1) * PIECE], result[:])
+            nc.sync.dma_start(out_rows[:, :, c * CHUNK : (c + 1) * CHUNK], result[:])
 
-        def decode_last(c):
-            for h, copy in enumerate((nc.scalar.copy, nc.vector.tensor_copy)):
-                acc = psum.tile([P, PIECE], F32, name=("yd", "y")[h])
-                product(acc[:], w4_q, slice(h * P, (h + 1) * P), hid_q[c])
-                result = held.tile([P, PIECE], F32, name=f"result{c}_{h}")
-                copy(result[:], acc[:])
-                nc.sync.dma_start(out_rows[:, h, c * PIECE : (c + 1) * PIECE], result[:])
+        def decode_half(c, h, tag, copy):
+            acc = psum.tile([P, CHUNK], F32, name=tag)
+            product(acc[:], w4_q[h], hid_q[c])
+            result = held.tile([P, CHUNK], F32, name=f"result{c}_{h}")
+            copy(result[:], acc[:])
+            nc.sync.dma_start(out_rows[:, h, c * CHUNK : (c + 1) * CHUNK], result[:])
 
-        weave(last)
-        weave(0)
-        for c in range(1, last):
-            weave(c)
+        interleave(LAST_CHUNK)
+        interleave(0)
+        for c in range(1, LAST_CHUNK):
+            interleave(c)
             quantise_hid(c - 1)
-        quantise_hid(last - 1)
-        quantise_hid(last)
-        for c in range(last):
-            decode(c)
-        decode_last(last)
+        quantise_hid(LAST_CHUNK - 1)
+        quantise_hid(LAST_CHUNK)
+        for c, tag in enumerate(("acc", "acc", "ye")):
+            decode(c, tag)
+        decode_half(LAST_CHUNK, 0, "yd", nc.scalar.copy)
+        decode_half(LAST_CHUNK, 1, "y", nc.vector.tensor_copy)

@@ -20,6 +20,7 @@ COPY = mybir.ActivationFunctionType.Copy
 P = 128
 PACK = 4
 LAST_TILE = PACK - 1
+EARLY = 2
 QUADRANT = 32
 PER_COLUMN = 16
 RUN = 4
@@ -66,7 +67,7 @@ def tile_picked_yblshap_cor_p_kernel(
         def load_row_tiles(name, w, t0, count):
             rows = held.tile([P, count, S], F32, name=f"{name}{t0}")
             nc.sync.dma_start(rows[:], w.rearrange("(p t) c -> p t c", t=PACK)[:, t0 : t0 + count, :])
-            return [rows[:, t, :] for t in range(count)]
+            return rows
 
         e_scale_tile = zeroed_scale_tile("e_scale_tile", e_scales)
         d_scale_tile = zeroed_scale_tile("d_scale_tile", d_scales)
@@ -82,21 +83,21 @@ def tile_picked_yblshap_cor_p_kernel(
         w3_raw = load_weight("w3_raw", w3)
         unit_rows = held.tile([P, PACK], F32, name="unit_rows")
         nc.sync.dma_start(unit_rows[:], unit.rearrange("(p t) o -> p (t o)", t=PACK))
-        wa_rows = load_row_tiles("wa", wa, 0, 1)
-        wb_rows = load_row_tiles("wb", wb, 0, 1)
+        wa_0 = load_row_tiles("wa", wa, 0, 1)
+        wb_0 = load_row_tiles("wb", wb, 0, 1)
         offs_list = load_list("offs_list", offs)
         x_word_tile = load_words("x_word_tile", x_words)
         load_scales(x_scale_tile, x_scales, X_FIRST)
         w1_raw = load_weight("w1_raw", w1)
         cor_list = load_list("cor_list", cor)
-        wa_rows.extend(load_row_tiles("wa", wa, 1, 1))
-        wb_rows.extend(load_row_tiles("wb", wb, 1, 1))
+        wa_1 = load_row_tiles("wa", wa, 1, 1)
+        wb_1 = load_row_tiles("wb", wb, 1, 1)
         vt_list = load_list("vt_list", vt)
-        wa_rows.extend(load_row_tiles("wa", wa, 2, 1))
-        wb_rows.extend(load_row_tiles("wb", wb, 2, 1))
-        wa_rows.extend(load_row_tiles("wa", wa, 3, 1))
-        wb_rows.extend(load_row_tiles("wb", wb, 3, 1))
+        wa_late = load_row_tiles("wa", wa, EARLY, PACK - EARLY)
+        wb_late = load_row_tiles("wb", wb, EARLY, PACK - EARLY)
         w4_raw = load_weight("w4_raw", w4)
+        wa_rows = [wa_0[:, 0, :], wa_1[:, 0, :], wa_late[:, 0, :], wa_late[:, 1, :]]
+        wb_rows = [wb_0[:, 0, :], wb_1[:, 0, :], wb_late[:, 0, :], wb_late[:, 1, :]]
 
 
         def pick(name, word_tile, scale_tile, first, offsets):
@@ -144,21 +145,36 @@ def tile_picked_yblshap_cor_p_kernel(
             product(acc[:], stationary, moving)
             nc.vector.scalar_tensor_tensor(result, acc[:], unit_rows[:, t : t + 1], other, MULT, op)
 
+        def term_tiles(t):
+            if t == EARLY:
+                pair = held.tile([P, 2, S], F32, name=f"term_e{t - 1}")
+                term_e[t], term_d[t] = pair[:, 0, :], pair[:, 1, :]
+            else:
+                first = held.tile([P, S], F32, name=f"term_e{t}")
+                second = held.tile([P, S], F32, name=f"term_d{t}")
+                term_e[t], term_d[t] = first[:], second[:]
+
         def first_shape(t):
-            term_e[t] = held.tile([P, S], F32, name=f"term_e{t}")
-            weighted_product("ye", w2_q[t], e_picked, t, term_e[t][:], wa_rows[t], MULT)
+            term_tiles(t)
+            weighted_product("ye", w2_q[t], e_picked, t, term_e[t], wa_rows[t], MULT)
 
         def second_shape(t):
-            term_d[t] = held.tile([P, S], F32, name=f"term_d{t}")
-            weighted_product("yd", w3_q[t], d_picked, t, term_d[t][:], wb_rows[t], MULT)
+            weighted_product("yd", w3_q[t], d_picked, t, term_d[t], wb_rows[t], MULT)
 
         def both_weights(t):
-            both[t] = held.tile([P, S], F32, name=f"both{t}")
-            nc.vector.tensor_tensor(both[t][:], wa_rows[t], wb_rows[t], MULT)
+            tile = held.tile([P, S], F32, name=f"both{t}")
+            nc.vector.tensor_tensor(tile[:], wa_rows[t], wb_rows[t], MULT)
+            both[t] = tile[:]
+
+        def both_weights_late():
+            pair = held.tile([P, PACK - EARLY, S], F32, name=f"term_d{EARLY - 1}")
+            nc.gpsimd.tensor_tensor(pair[:], wa_late[:], wb_late[:], MULT)
+            for t in range(EARLY, PACK):
+                both[t] = pair[:, t - EARLY, :]
 
         def sum_shapes(t):
             blend_tile[t] = held.tile([P, 2 * S], F32, name=f"blend{t}")
-            nc.vector.tensor_tensor(blend_tile[t][:, S:], term_e[t][:], term_d[t][:], ADD)
+            nc.vector.tensor_tensor(blend_tile[t][:, S:], term_e[t], term_d[t], ADD)
 
         def blend(t):
             weighted_product("y", w1_q[t], x_picked, t, blend_tile[t][:, :S], blend_tile[t][:, S:], ADD)
@@ -166,11 +182,11 @@ def tile_picked_yblshap_cor_p_kernel(
         def corrective(t):
             fixed_tile[t] = held.tile([P, 2 * S], F32, name=f"fixed{t}")
             other_vertex = blend_tile[t][:].indirect(cor_list[:])
-            if t != LAST_TILE:
+            if t < EARLY:
                 fetched = held.tile([P, S], F32, name=f"fetched{t}")
                 nc.scalar.activation(fetched[:], other_vertex, COPY)
                 other_vertex = fetched[:]
-            nc.vector.tensor_tensor(fixed_tile[t][:, S:], other_vertex, both[t][:], MULT)
+            nc.vector.tensor_tensor(fixed_tile[t][:, S:], other_vertex, both[t], MULT)
 
         def fix(t):
             nc.vector.tensor_tensor(fixed_tile[t][:, :S], blend_tile[t][:, :S], fixed_tile[t][:, S:], SUB)
@@ -203,32 +219,32 @@ def tile_picked_yblshap_cor_p_kernel(
         second_shape(0)
         first_shape(1)
         sum_shapes(0)
-        w1_q = quantise_dealt("w1", w1_raw, 0, 2)
+        w1_q = quantise_dealt("w1", w1_raw, 0, EARLY)
         second_shape(1)
         both_weights(1)
-        blend(0)
-        w1_q.extend(quantise_dealt("w1", w1_raw, 2, 2))
+        w1_q.extend(quantise_dealt("w1", w1_raw, EARLY, PACK - EARLY))
         sum_shapes(1)
-        corrective(0)
+
+        both_weights_late()
+        blend(0)
         blend(1)
         first_shape(2)
         second_shape(2)
-        fix(0)
-        both_weights(2)
+        corrective(0)
         sum_shapes(2)
+        fix(0)
         corrective(1)
         look_up(0)
         blend(2)
         first_shape(3)
         fix(1)
+        look_up(1)
         w4_q = quantise_w4()
         second_shape(3)
         corrective(2)
-        look_up(1)
         sum_shapes(3)
         fix(2)
         look_up(2)
-        both_weights(3)
         blend(3)
         corrective(3)
         fix(3)

from contextlib import ExitStack

import concourse.mybir as mybir

K, H, S, U, N = 512, 512, 512, 1024, 256
FLOPS = 3 * 2 * K * H * S + 2 * H * N * U

F32 = mybir.dt.float32
BF16 = mybir.dt.bfloat16
I32 = mybir.dt.int32
U32 = mybir.dt.uint32
U16 = mybir.dt.uint16
U8 = mybir.dt.uint8
FP8X4 = mybir.dt.float8_e4m3fn_x4
MULT = mybir.AluOpType.mult
ADD = mybir.AluOpType.add
SUB = mybir.AluOpType.subtract
COPY = mybir.ActivationFunctionType.Copy

P = 128
PACK = 4
LAST_TILE = PACK - 1
EARLY = 2
QUADRANT = 32
PER_COLUMN = 16
RUN = 4
CHUNK = 256
CHUNKS = U // CHUNK
LAST_CHUNK = CHUNKS - 1
E_FIRST, D_FIRST, X_FIRST = 0, 4, 8


def tile_picked_yblshap_cor_p_kernel(
    tc, x_words, x_scales, w1, e_words, e_scales, w2, d_words, d_scales, w3, wa, wb, unit, w4, offs, bsa, bsb, cor, vt, out
):
    nc = tc.nc
    with ExitStack() as ctx:
        held = ctx.enter_context(tc.tile_pool(name="held", bufs=1))
        psum = ctx.enter_context(tc.psum_pool(name="psum", bufs=2))


        def load_list(name, src):
            tile = held.tile(list(src.shape), U16, name=name)
            nc.sync.dma_start(tile[:], src)
            return tile

        def load_words(name, words):
            tile = held.tile([P, words.shape[2]], I32, name=name, align_bytes=64)
            nc.sync.dma_start(tile[:], words[0].rearrange("p n r -> p (n r)").bitcast(I32))
            return tile

        def zeroed_scale_tile(name, scales):
            tile = held.tile([P, scales.shape[2]], U8, name=name, align_bytes=64)
            nc.vector.memset(tile[:].bitcast(I32), 0)
            return tile

        def load_scales(tile, scales, first):
            for q in range(P // QUADRANT):
                p0 = QUADRANT * q + first
                nc.sync.dma_start(tile[p0 : p0 + 4, :].bitcast(I32), scales[0, 4 * q : 4 * q + 4, :].bitcast(I32))

        def load_weight(name, w):
            raw = held.tile([P, PACK, w.shape[1]], F32, name=name)
            nc.sync.dma_start(raw[:], w.rearrange("(p j) c -> p j c", j=PACK))
            return raw

        def load_row_tiles(name, w, t0, count):
            rows = held.tile([P, count, S], F32, name=f"{name}{t0}")
            nc.sync.dma_start(rows[:], w.rearrange("(p t) c -> p t c", t=PACK)[:, t0 : t0 + count, :])
            return rows

        e_scale_tile = zeroed_scale_tile("e_scale_tile", e_scales)
        d_scale_tile = zeroed_scale_tile("d_scale_tile", d_scales)
        x_scale_tile = zeroed_scale_tile("x_scale_tile", x_scales)

        bsa_list = load_list("bsa_list", bsa)
        e_word_tile = load_words("e_word_tile", e_words)
        load_scales(e_scale_tile, e_scales, E_FIRST)
        w2_raw = load_weight("w2_raw", w2)
        d_word_tile = load_words("d_word_tile", d_words)
        bsb_list = load_list("bsb_list", bsb)
        load_scales(d_scale_tile, d_scales, D_FIRST)
        w3_raw = load_weight("w3_raw", w3)
        unit_rows = held.tile([P, PACK], F32, name="unit_rows")
        nc.sync.dma_start(unit_rows[:], unit.rearrange("(p t) o -> p (t o)", t=PACK))
        wa_0 = load_row_tiles("wa", wa, 0, 1)
        wb_0 = load_row_tiles("wb", wb, 0, 1)
        offs_list = load_list("offs_list", offs)
        x_word_tile = load_words("x_word_tile", x_words)
        load_scales(x_scale_tile, x_scales, X_FIRST)
        w1_raw = load_weight("w1_raw", w1)
        cor_list = load_list("cor_list", cor)
        wa_1 = load_row_tiles("wa", wa, 1, 1)
        wb_1 = load_row_tiles("wb", wb, 1, 1)
        vt_list = load_list("vt_list", vt)
        wa_late = load_row_tiles("wa", wa, EARLY, PACK - EARLY)
        wb_late = load_row_tiles("wb", wb, EARLY, PACK - EARLY)
        w4_raw = load_weight("w4_raw", w4)
        wa_rows = [wa_0[:, 0, :], wa_1[:, 0, :], wa_late[:, 0, :], wa_late[:, 1, :]]
        wb_rows = [wb_0[:, 0, :], wb_1[:, 0, :], wb_late[:, 0, :], wb_late[:, 1, :]]


        def pick(name, word_tile, scale_tile, first, offsets):
            words = held.tile([P, S], U32, name=name + "_words", align_bytes=64)
            nc.vector.tensor_copy(words[:], word_tile[:].bitcast(U32).indirect(offsets[:]))
            scales = held.tile([P, S], U8, name=name + "_scales", align_bytes=64)
            nc.vector.tensor_copy(scales[:], scale_tile[:].indirect(offsets[:]))
            return words[:], scales[first:P, :]

        def quantise(name, grouped):
            width = grouped.shape[1] // PACK
            words = held.tile([P, width], U32, name=name + "_words", align_bytes=64)
            scales = held.tile([P, width], U8, name=name + "_scales", align_bytes=64)
            nc.vector.quantize_mx(out=words[:].bitcast(FP8X4), scales=scales[:], in_=grouped)
            return words[:], scales[:]

        def quantise_dealt(name, raw, t0, count):
            grouped = held.tile([P, count * P * PACK], BF16, name=f"{name}_bf{t0}", align_bytes=64)
            nc.scalar.activation(
                grouped[:].rearrange("p (t m j) -> p m j t", t=count, j=PACK),
                raw[:].rearrange("p j (m t) -> p m j t", t=PACK)[:, :, :, t0 : t0 + count],
                COPY,
            )
            return split_stationary(quantise(f"{name}_{t0}", grouped[:]))

        def split_stationary(operand):
            words, scales = operand
            return [(words[:, c : c + P], scales[:, c : c + P]) for c in range(0, words.shape[1], P)]

        def product(acc, stationary, moving):
            nc.tensor.matmul_mx(
                out=acc,
                lhsT=stationary[0].bitcast(FP8X4),
                lhsT_scale=stationary[1],
                rhs=moving[0].bitcast(FP8X4),
                rhs_scale=moving[1],
                start=True,
                stop=True,
            )

        term_e, term_d, both, blend_tile, fixed_tile = {}, {}, {}, {}, {}

        def weighted_product(tag, stationary, moving, t, result, other, op):
            acc = psum.tile([P, S], F32, name=tag)
            product(acc[:], stationary, moving)
            nc.vector.scalar_tensor_tensor(result, acc[:], unit_rows[:, t : t + 1], other, MULT, op)

        def term_tiles(t):
            if t == EARLY:
                pair = held.tile([P, 2, S], F32, name=f"term_e{t - 1}")
                term_e[t], term_d[t] = pair[:, 0, :], pair[:, 1, :]
            else:
                first = held.tile([P, S], F32, name=f"term_e{t}")
                second = held.tile([P, S], F32, name=f"term_d{t}")
                term_e[t], term_d[t] = first[:], second[:]

        def first_shape(t):
            term_tiles(t)
            weighted_product("ye", w2_q[t], e_picked, t, term_e[t], wa_rows[t], MULT)

        def second_shape(t):
            weighted_product("yd", w3_q[t], d_picked, t, term_d[t], wb_rows[t], MULT)

        def both_weights(t):
            tile = held.tile([P, S], F32, name=f"both{t}")
            nc.vector.tensor_tensor(tile[:], wa_rows[t], wb_rows[t], MULT)
            both[t] = tile[:]

        def both_weights_late():
            pair = held.tile([P, PACK - EARLY, S], F32, name=f"term_d{EARLY - 1}")
            nc.gpsimd.tensor_tensor(pair[:], wa_late[:], wb_late[:], MULT)
            for t in range(EARLY, PACK):
                both[t] = pair[:, t - EARLY, :]

        def sum_shapes(t):
            blend_tile[t] = held.tile([P, 2 * S], F32, name=f"blend{t}")
            nc.vector.tensor_tensor(blend_tile[t][:, S:], term_e[t], term_d[t], ADD)

        def blend(t):
            weighted_product("y", w1_q[t], x_picked, t, blend_tile[t][:, :S], blend_tile[t][:, S:], ADD)

        def corrective(t):
            fixed_tile[t] = held.tile([P, 2 * S], F32, name=f"fixed{t}")
            other_vertex = blend_tile[t][:].indirect(cor_list[:])
            if t < EARLY:
                fetched = held.tile([P, S], F32, name=f"fetched{t}")
                nc.scalar.activation(fetched[:], other_vertex, COPY)
                other_vertex = fetched[:]
            nc.vector.tensor_tensor(fixed_tile[t][:, S:], other_vertex, both[t], MULT)

        def fix(t):
            nc.vector.tensor_tensor(fixed_tile[t][:, :S], blend_tile[t][:, :S], fixed_tile[t][:, S:], SUB)

        hid_rows = [held.tile([P, PACK, U // 2], BF16, name=f"hid_rows{half}", align_bytes=64) for half in range(2)]

        def look_up(t):
            width = CHUNK if t == LAST_TILE else U // 2
            for r0 in range(0, U, width):
                corners = fixed_tile[t][:].indirect(vt_list[:, r0 // PER_COLUMN : (r0 + width) // PER_COLUMN])
                half, c0 = divmod(r0, U // 2)
                nc.scalar.activation(hid_rows[half][:, t, c0 : c0 + width], corners, COPY)

        def quantise_w4():
            grouped = held.tile([P, N, PACK], BF16, name="w4_bf", align_bytes=64)
            nc.scalar.activation(
                grouped[:].rearrange("p (c i) j -> p c j i", i=RUN),
                w4_raw[:].rearrange("p j (c i) -> p c j i", i=RUN),
                COPY,
            )
            return split_stationary(quantise("w4", grouped[:].rearrange("p c j -> p (c j)")))

        e_picked = pick("e_picked", e_word_tile, e_scale_tile, E_FIRST, bsa_list)
        d_picked = pick("d_picked", d_word_tile, d_scale_tile, D_FIRST, bsb_list)
        w2_q = quantise_dealt("w2", w2_raw, 0, PACK)
        both_weights(0)
        first_shape(0)
        w3_q = quantise_dealt("w3", w3_raw, 0, PACK)
        x_picked = pick("x_picked", x_word_tile, x_scale_tile, X_FIRST, offs_list)
        second_shape(0)
        first_shape(1)
        sum_shapes(0)
        w1_q = quantise_dealt("w1", w1_raw, 0, EARLY)
        second_shape(1)
        both_weights(1)
        w1_q.extend(quantise_dealt("w1", w1_raw, EARLY, PACK - EARLY))
        sum_shapes(1)

        both_weights_late()
        blend(0)
        blend(1)
        first_shape(2)
        second_shape(2)
        corrective(0)
        sum_shapes(2)
        fix(0)
        corrective(1)
        look_up(0)
        blend(2)
        first_shape(3)
        fix(1)
        look_up(1)
        w4_q = quantise_w4()
        second_shape(3)
        corrective(2)
        sum_shapes(3)
        fix(2)
        look_up(2)
        blend(3)
        corrective(3)
        fix(3)
        look_up(3)

        out_rows = out.rearrange("(h p) r -> p h r", p=P)
        hid_grouped, hid_q = {}, {}

        def interleave(c):
            half, c0 = divmod(c * CHUNK, U // 2)
            hid_grouped[c] = held.tile([P, CHUNK, PACK], BF16, name=f"hid_grouped{c}", align_bytes=64)
            copy = nc.scalar.copy if c == LAST_CHUNK else nc.vector.tensor_copy
            copy(
                hid_grouped[c][:].rearrange("p (r i) t -> p r t i", i=RUN),
                hid_rows[half][:, :, c0 : c0 + CHUNK].rearrange("p t (r i) -> p r t i", i=RUN),
            )

        def quantise_hid(c):
            hid_q[c] = quantise(f"hid{c}", hid_grouped[c][:].rearrange("p r t -> p (r t)"))

        def decode(c, tag):
            acc = psum.tile([P, N // P, CHUNK], F32, name=tag)
            for h in range(N // P):
                product(acc[:, h, :], w4_q[h], hid_q[c])
            result = held.tile([P, N // P, CHUNK], F32, name=f"result{c}")
            nc.scalar.copy(result[:], acc[:])
            nc.sync.dma_start(out_rows[:, :, c * CHUNK : (c + 1) * CHUNK], result[:])

        def decode_half(c, h, tag, copy):
            acc = psum.tile([P, CHUNK], F32, name=tag)
            product(acc[:], w4_q[h], hid_q[c])
            result = held.tile([P, CHUNK], F32, name=f"result{c}_{h}")
            copy(result[:], acc[:])
            nc.sync.dma_start(out_rows[:, h, c * CHUNK : (c + 1) * CHUNK], result[:])

        interleave(LAST_CHUNK)
        interleave(0)
        for c in range(1, LAST_CHUNK):
            interleave(c)
            quantise_hid(c - 1)
        quantise_hid(LAST_CHUNK - 1)
        quantise_hid(LAST_CHUNK)
        for c, tag in enumerate(("acc", "acc", "ye")):
            decode(c, tag)
        decode_half(LAST_CHUNK, 0, "yd", nc.scalar.copy)
        decode_half(LAST_CHUNK, 1, "y", nc.vector.tensor_copy)
